import numpy as np
import ml_dtypes


def mxq(x, axis, fmt="e4m3"):
    dtype, down = {"e4m3": (ml_dtypes.float8_e4m3fn, 7), "e5m2": (ml_dtypes.float8_e5m2, 14)}[fmt]
    v = np.moveaxis(np.asarray(x, np.float32).astype(ml_dtypes.bfloat16).astype(np.float64), axis, -1)
    blocks = v.reshape(v.shape[:-1] + (-1, 32))
    amax = np.abs(blocks).max(-1, keepdims=True)
    byte = np.maximum(np.where(amax > 0, np.frexp(amax)[1] - 1 + 127, 0) - down, 1)
    scale = np.exp2(byte - 127.0)
    codes = (blocks / scale).astype(np.float32).astype(dtype).astype(np.float64)
    return np.moveaxis((codes * scale).reshape(v.shape), -1, axis)


WIDE = False


def mx_kscale(k):
    if not WIDE:
        return np.ones(k)
    levels = np.array([10, -10, 5, -5, 0])
    if k % 512:
        return np.exp2(np.random.permutation(np.resize(levels, k // 32))).repeat(32)
    a = np.empty((k // 512, 16))
    for p in range(k // 512):
        a[p, :8] = np.random.permutation(np.resize(levels, 8))
        for g in range(8):
            far = levels[np.abs(levels - a[p, g]) >= 10]
            a[p, g + 8] = far[np.random.randint(len(far))]
    return np.exp2(a.ravel()).repeat(32)


def f64(x):
    return np.asarray(x).astype(np.float64)


def striped(idx):
    return np.tile(idx.reshape(-1, 16).T, (8, 1)).astype(np.uint16)


def unstriped(offs):
    return offs[:16].T.reshape(-1).astype(np.int64)


def striped8(idx):
    return np.concatenate([x.reshape(-1, 16).T for x in idx]).astype(np.uint16)


def runs(offs, k):
    lists = np.stack([offs[16 * r : 16 * r + 16].T.reshape(-1) for r in range(8)]).astype(np.int64)
    return lists[np.arange(k) % 512 // 64]


def pack_weight(w):
    k, n = w.shape
    w = f64(np.asarray(w, np.float32).astype(ml_dtypes.bfloat16)).reshape(k // 32, 32, n)
    amax = np.abs(w).max(1)
    byte = np.clip(np.where(amax > 0, np.frexp(amax)[1] - 1 + 127 - 7, 1), 1, 254)
    scaled = (w * np.exp2(127.0 - byte)[:, None, :]).reshape(k, n).astype(np.float32)
    words = np.ascontiguousarray(scaled.reshape(k // 512, 128, 4, n).transpose(0, 1, 3, 2)).astype(ml_dtypes.float8_e4m3fn).view(np.uint8)
    return words, np.ascontiguousarray(byte.astype(np.uint8).reshape(k // 512, 16, n))


def unpack_weight(words, scales):
    g, p, n, _ = words.shape
    vals = np.ascontiguousarray(words).view(ml_dtypes.float8_e4m3fn).astype(np.float64) * np.repeat(np.exp2(scales.astype(np.float64) - 127.0), 8, axis=1)[..., None]
    return vals.transpose(0, 1, 3, 2).reshape(g * 512, n)


E2M1 = np.array([0.0, 0.5, 1.0, 1.5, 2.0, 3.0, 4.0, 6.0, -0.0, -0.5, -1.0, -1.5, -2.0, -3.0, -4.0, -6.0])


def pack_fp4(w):
    k, n = w.shape
    w = f64(np.asarray(w, np.float32).astype(ml_dtypes.bfloat16)).reshape(k // 32, 32, n)
    amax = np.abs(w).max(1)
    mant, ex = np.frexp(amax / 6.0)
    byte = np.clip(np.where(amax > 0, np.where(mant > 0.5, ex, ex - 1) + 127, 1), 1, 254)
    scaled = (w * np.exp2(127.0 - byte)[:, None, :]).reshape(k, n).astype(np.float32)
    c = np.ascontiguousarray(scaled.reshape(k // 512, 128, 4, n).transpose(0, 1, 3, 2)).astype(ml_dtypes.float4_e2m1fn).view(np.uint8) & 0xF
    words = (c[..., 0::2] | (c[..., 1::2] << 4)).reshape(k // 512, 128, 2 * n)
    return np.ascontiguousarray(words), np.ascontiguousarray(byte.astype(np.uint8).reshape(k // 512, 16, n))


def unpack_fp4(words, scales):
    g, _, n = scales.shape
    words = np.ascontiguousarray(words).reshape(g, 128, n, 2)
    nib = np.empty((g, 128, n, 4), np.uint8)
    nib[..., 0::2] = words & 0xF
    nib[..., 1::2] = words >> 4
    vals = E2M1[nib] * np.repeat(np.exp2(scales.astype(np.float64) - 127.0), 8, axis=1)[..., None]
    return vals.transpose(0, 1, 3, 2).reshape(g * 512, n)


def relu(v):
    return np.maximum(v, 0.0)

def planes(y):
    n, m = y.shape
    v = y.astype(np.float32).astype(ml_dtypes.bfloat16).astype(np.float64).reshape(n // 32, 32, m)
    top = np.abs(v).max(1)
    byte = np.clip(np.where(top > 0, np.frexp(top)[1] - 1 + 127 - 7, 1), 1, 254)
    codes = (v * np.exp2(127.0 - byte)[:, None, :]).reshape(n, m).astype(np.float32).astype(ml_dtypes.float8_e4m3fn).view(np.uint8)
    words = codes.reshape(n // 512, 128, 4, m).transpose(0, 1, 3, 2)
    return np.ascontiguousarray(words), np.ascontiguousarray(byte.astype(np.uint8).reshape(n // 512, 16, m))


K, T, S, V, N, H = 512, 2048, 512, 256, 512, 512


def setup_inputs():
    n = np.random.standard_normal
    s = mx_kscale(K)[:, None]
    u = mx_kscale(H)
    packed_xT = pack_weight(n((K, T)) * s)
    packed_w3 = pack_fp4(n((H, N)) / np.sqrt(H) / u[:, None])
    perm = np.stack([np.random.permutation(S) for _ in range(8)])
    return {
        "x_words": packed_xT[0],
        "x_scales": packed_xT[1],
        "w1": (n((K, H)) / np.sqrt(K) / s * u).astype(np.float32),
        "w2": (n((H, H)) / np.sqrt(H) / u[:, None] * u).astype(np.float32),
        "w3_words": packed_w3[0],
        "w3_scales": packed_w3[1],
        "offs": striped(np.random.permutation(T)[:S]),
        "la": striped8(perm[:, :V]),
        "lb": striped8(perm[:, V:]),
    }


def reference(x_words, x_scales, w1, w2, w3_words, w3_scales, offs, la, lb):
    xq = unpack_weight(x_words, x_scales)[:, unstriped(offs)]
    y = mxq(f64(w1), 0, "e4m3").T @ xq
    a = y[np.arange(H)[:, None], runs(la, H)]
    b = y[np.arange(H)[:, None], runs(lb, H)]
    z = 0.75 * (a + b)
    h = relu(mxq(f64(w2), 0, "e4m3").T @ mxq(z, 0, "e4m3"))
    df = a - b
    hb = h - df
    ha = h + df
    p = np.zeros((H, S))
    p[np.arange(H)[:, None], runs(la, H)] = ha
    z2 = p.copy()
    z2[np.arange(H)[:, None], runs(lb, H)] = hb
    out_0 = unpack_fp4(w3_words, w3_scales).T @ mxq(z2, 0, "e4m3")
    return (out_0,) + planes(out_0)

@@ -1,0 +1,248 @@
+from contextlib import ExitStack
+
+import concourse.mybir as mybir
+
+K, T, S, V, N, H = 512, 2048, 512, 256, 512, 512
+FLOPS = 2 * K * H * S + 2 * H * H * V + 2 * H * N * S
+
+F32 = mybir.dt.float32
+BF16 = mybir.dt.bfloat16
+I32 = mybir.dt.int32
+U32 = mybir.dt.uint32
+U16 = mybir.dt.uint16
+U8 = mybir.dt.uint8
+FP8X4 = mybir.dt.float8_e4m3fn_x4
+FP4X4 = mybir.dt.float4_e2m1fn_x4
+ALU = mybir.AluOpType
+ACT = mybir.ActivationFunctionType
+
+P = 128
+PACK = 4
+CHUNK = 128
+
+
+def tile_picked_unmerge_relu_po_kernel(
+    tc, x_words, x_scales, w1, w2, w3_words, w3_scales, offs, la, lb, out_0, out_1, out_2
+):
+    nc = tc.nc
+    with ExitStack() as ctx:
+        keep = ctx.enter_context(tc.tile_pool(name="keep", bufs=1))
+        psum = ctx.enter_context(tc.psum_pool(name="psum", bufs=1))
+
+        def sb(name, shape, dtype, tag=None):
+            return keep.tile(shape, dtype, name=name, tag=tag or name, align_bytes=64)
+
+        def bank(number, name, shape):
+            return psum.tile(shape, F32, name=name, tag=f"bank{number}")
+
+        def load_scale_rows(queue, tile, rows):
+            for q in range(4):
+                queue.dma_start(out=tile[32 * q : 32 * q + 4, :].bitcast(I32), in_=rows[4 * q : 4 * q + 4, :].bitcast(I32))
+
+        offs_sb = keep.tile([P, S // 16], U16, name="offs_sb")
+        la_sb = keep.tile([P, V // 16], U16, name="la_sb")
+        lb_sb = keep.tile([P, V // 16], U16, name="lb_sb")
+        xw = sb("xw", [P, T], U32)
+        xs = sb("xs", [P, T], U8)
+        w1_raw = sb("w1_raw", [P, PACK, H], F32, "w_raw")
+        w3s_raw = sb("w3s_raw", [P, N], U8)
+
+        nc.vector.memset(xs[:].bitcast(I32), 0)
+        nc.gpsimd.memset(w3s_raw[:].bitcast(I32), 0)
+        load_scale_rows(nc.gpsimd, w3s_raw, w3_scales[0])
+        nc.sync.dma_start(offs_sb[:], offs)
+        nc.sync.dma_start(out=w1_raw[:], in_=w1.rearrange("(p j) c -> p j c", j=PACK))
+        nc.sync.dma_start(la_sb[:], la)
+        nc.sync.dma_start(lb_sb[:], lb)
+        nc.sync.dma_start(out=xw[:].bitcast(I32), in_=x_words[0].rearrange("p n t -> p (n t)").bitcast(I32))
+        load_scale_rows(nc.scalar, xs, x_scales[0])
+
+        def deal(engine, raw, name, pair):
+            grouped = sb(name, [P, 2, P, PACK], BF16)
+            dst = grouped[:].rearrange("p t m j -> p m j t")
+            src = raw[:].rearrange("p j (m t) -> p m j t", t=PACK)[:, :, :, 2 * pair : 2 * pair + 2]
+            if engine is nc.vector:
+                nc.vector.tensor_copy(out=dst, in_=src)
+            else:
+                nc.scalar.copy(out=dst, in_=src)
+            return grouped
+
+        def quantise(name, values, width):
+            codes = sb(name + "_codes", [P, width], U32)
+            scales = sb(name + "_scales", [P, width], U8)
+            nc.vector.quantize_mx(out=codes[:].bitcast(FP8X4), scales=scales[:], in_=values)
+            return codes, scales
+
+        xsg = sb("xsg", [P, S], U8)
+        g1 = [deal(nc.vector, w1_raw, "w1_g0", 0), deal(nc.scalar, w1_raw, "w1_g1", 1)]
+        q1 = [quantise("w1_q0", g1[0][:].rearrange("p t m j -> p (t m j)"), 2 * P)]
+        nc.vector.tensor_copy(out=xsg[:], in_=xs[:].indirect(offs_sb[:]))
+        q1.append(quantise("w1_q1", g1[1][:].rearrange("p t m j -> p (t m j)"), 2 * P))
+
+        w3w_raw = sb("w3w_raw", [P, 2 * N], U8, "w1_g0")
+        nc.sync.dma_start(out=w3w_raw[:].bitcast(I32), in_=w3_words[0].bitcast(I32))
+        w2_raw = sb("w2_raw", [P, PACK, H], F32, "w_raw")
+        nc.sync.dma_start(out=w2_raw[:], in_=w2.rearrange("(p j) c -> p j c", j=PACK))
+
+        half = S // 2
+        xg = [sb("xg0", [P, half], U32, "xs"), sb("xg1", [P, half], U32)]
+        for u in range(2):
+            nc.vector.tensor_copy(out=xg[u][:], in_=xw[:].indirect(offs_sb[:, 16 * u : 16 * u + 16]))
+
+        y = [sb(f"y{t}", [P, S], F32) for t in range(PACK)]
+        for t, u in [(0, 0), (1, 0), (0, 1), (1, 1), (2, 0), (2, 1), (3, 0), (3, 1)]:
+            codes, scales = q1[t // 2]
+            cols = slice(P * (t % 2), P * (t % 2) + P)
+            acc = bank(2 * t + u, f"y_acc{t}{u}", [P, half])
+            nc.tensor.matmul_mx(
+                out=acc[:],
+                lhsT=codes[:, cols].bitcast(FP8X4),
+                lhsT_scale=scales[:, cols],
+                rhs=xg[u][:].bitcast(FP8X4),
+                rhs_scale=xsg[:, half * u : half * u + half],
+                start=True,
+                stop=True,
+            )
+            nc.scalar.copy(out=y[t][:, half * u : half * u + half], in_=acc[:])
+
+        w3w = sb("w3w", [P, PACK, P, 2], U8)
+        w3s = sb("w3s", [P, PACK, P], U8)
+        nc.vector.tensor_copy(
+            out=w3w[:].rearrange("p t m b -> p m t b"), in_=w3w_raw[:].rearrange("p (m t b) -> p m t b", t=PACK, b=2)
+        )
+        nc.vector.tensor_copy(out=w3s[:].rearrange("p t m -> p m t"), in_=w3s_raw[:].rearrange("p (m t) -> p m t", t=PACK))
+
+        vh = V // 2
+        a = [sb(f"a{g}", [P, PACK, vh], F32) for g in range(2)]
+        s = [sb(f"s{g}", [P, PACK, vh], F32) for g in range(2)]
+        df = sb("df", [P, PACK, V], F32)
+        ndf = sb("ndf", [P, PACK, V], F32)
+        h = sb("h", [P, PACK, V], F32)
+
+        def gather(g, t):
+            lists = slice(8 * g, 8 * g + 8)
+            nc.vector.tensor_copy(out=a[g][:, t, :], in_=y[t][:].indirect(la_sb[:, lists]))
+
+        def gather_add(g, t):
+            lists = slice(8 * g, 8 * g + 8)
+            nc.vector.tensor_tensor(out=s[g][:, t, :], in0=y[t][:].indirect(lb_sb[:, lists]), in1=a[g][:, t, :], op=ALU.add)
+
+        def gathers(g, ts):
+            for t in ts:
+                gather(g, t)
+            for t in ts:
+                gather_add(g, t)
+
+        def merge(g):
+            zi = sb(f"zi{g}", [P, vh, PACK], BF16)
+            nc.scalar.activation(
+                out=zi[:].rearrange("p (c i) t -> p c t i", i=4),
+                in_=s[g][:].rearrange("p t (c i) -> p c t i", i=4),
+                func=ACT.Copy,
+                scale=0.75,
+            )
+            return zi
+
+        def second_layer(g, qz, q2):
+            acc = bank(g, f"h_acc{g}", [P, PACK, vh])
+            for t in range(PACK):
+                codes, scales = q2[t // 2]
+                cols = slice(P * (t % 2), P * (t % 2) + P)
+                nc.tensor.matmul_mx(
+                    out=acc[:, t, :],
+                    lhsT=codes[:, cols].bitcast(FP8X4),
+                    lhsT_scale=scales[:, cols],
+                    rhs=qz[0][:].bitcast(FP8X4),
+                    rhs_scale=qz[1][:],
+                    start=True,
+                    stop=True,
+                )
+            nc.scalar.activation(out=h[:, :, vh * g : vh * g + vh], in_=acc[:], func=ACT.Relu)
+
+        def difference(g):
+            cols = slice(vh * g, vh * g + vh)
+            nc.vector.scalar_tensor_tensor(
+                out=df[:, :, cols], in0=a[g][:], scalar=2.0, in1=s[g][:], op0=ALU.mult, op1=ALU.subtract
+            )
+
+        gathers(0, [0, 1])
+        gathers(0, [2, 3])
+        g2a = deal(nc.scalar, w2_raw, "w2_g0", 0)
+        zi0 = merge(0)
+        g2b = deal(nc.scalar, w2_raw, "w2_g1", 1)
+        gathers(1, [0, 1])
+        q2a = quantise("w2_q0", g2a[:].rearrange("p t m j -> p (t m j)"), 2 * P)
+        qz0 = quantise("z_q0", zi0[:].rearrange("p v t -> p (v t)"), vh)
+        gathers(1, [2, 3])
+        q2b = quantise("w2_q1", g2b[:].rearrange("p t m j -> p (t m j)"), 2 * P)
+        zi1 = merge(1)
+        second_layer(0, qz0, [q2a, q2b])
+        difference(0)
+        difference(1)
+        qz1 = quantise("z_q1", zi1[:].rearrange("p v t -> p (v t)"), vh)
+        second_layer(1, qz1, [q2a, q2b])
+        for u in range(2):
+            nc.scalar.activation(out=ndf[:, 2 * u : 2 * u + 2, :], in_=df[:, 2 * u : 2 * u + 2, :], func=ACT.Copy, scale=-1.0)
+
+        z2 = [sb(f"z2_{t}", [P, S], F32) for t in range(PACK)]
+        chunks = S // CHUNK
+        z2i = [sb(f"z2i{c}", [P, CHUNK, PACK], BF16) for c in range(chunks)]
+
+        def scatter(t, lists, term, lo, hi):
+            nc.vector.tensor_tensor(
+                out=z2[t][:].indirect(lists[:, lo // 16 : hi // 16]), in0=h[:, t, lo:hi], in1=term[:, t, lo:hi], op=ALU.add
+            )
+
+        def weave(t):
+            for c in range(chunks):
+                nc.scalar.copy(out=z2i[c][:, :, t], in_=z2[t][:, CHUNK * c : CHUNK * c + CHUNK])
+
+        scatter(0, la_sb, df, 0, vh)
+        scatter(1, la_sb, df, 0, vh)
+        scatter(0, la_sb, df, vh, V)
+        scatter(1, la_sb, df, vh, V)
+        scatter(0, lb_sb, ndf, 0, V)
+        weave(0)
+        scatter(2, la_sb, df, 0, V)
+        scatter(1, lb_sb, ndf, 0, V)
+        weave(1)
+        scatter(3, la_sb, df, 0, V)
+        scatter(2, lb_sb, ndf, 0, V)
+        weave(2)
+        scatter(3, lb_sb, ndf, 0, V)
+        weave(3)
+
+        out_rows = out_0.rearrange("(p t) j -> p t j", t=PACK)
+        word_rows = out_1[0].rearrange("p n t -> p (n t)").bitcast(I32)
+        o_codes = sb("o_codes", [P, S], U32)
+        o_scales = sb("o_scales", [P, S], U8)
+        qz2 = [quantise(f"z2_q{c}", z2i[c][:].rearrange("p v t -> p (v t)"), CHUNK) for c in range(chunks)]
+        for c in range(chunks):
+            cols = slice(CHUNK * c, CHUNK * c + CHUNK)
+            acc = bank(2 + c, f"o_acc{c}", [P, PACK, CHUNK])
+            for t in range(PACK):
+                nc.tensor.matmul_mx(
+                    out=acc[:, t, :],
+                    lhsT=w3w[:, t, :, :].rearrange("p m b -> p (m b)").bitcast(FP4X4),
+                    lhsT_scale=w3s[:, t, :],
+                    rhs=qz2[c][0][:].bitcast(FP8X4),
+                    rhs_scale=qz2[c][1][:],
+                    start=True,
+                    stop=True,
+                )
+            o = sb(f"o{c}", [P, PACK, CHUNK], F32)
+            nc.scalar.copy(out=o[:], in_=acc[:])
+            nc.sync.dma_start(out=out_rows[:, :, cols], in_=o[:])
+            oi = sb(f"oi{c}", [P, CHUNK, PACK], BF16)
+            nc.vector.tensor_copy(
+                out=oi[:].rearrange("p (c i) t -> p c t i", i=4), in_=o[:].rearrange("p t (c i) -> p c t i", i=4)
+            )
+            nc.vector.quantize_mx(
+                out=o_codes[:, cols].bitcast(FP8X4), scales=o_scales[:, cols], in_=oi[:].rearrange("p v t -> p (v t)")
+            )
+            nc.sync.dma_start(out=word_rows[:, cols], in_=o_codes[:, cols].bitcast(I32))
+        for q in range(4):
+            queue = nc.sync if q % 2 == 0 else nc.scalar
+            queue.dma_start(
+                out=out_2[0][4 * q : 4 * q + 4, :].bitcast(I32), in_=o_scales[32 * q : 32 * q + 4, :].bitcast(I32)
+            )

@@ -45,11 +45,8 @@ def tile_picked_unmerge_relu_po_kernel(
         xw = sb("xw", [P, T], U32)
         xs = sb("xs", [P, T], U8)
         w1_raw = sb("w1_raw", [P, PACK, H], F32, "w_raw")
-        w3s_raw = sb("w3s_raw", [P, N], U8)
 
         nc.vector.memset(xs[:].bitcast(I32), 0)
-        nc.gpsimd.memset(w3s_raw[:].bitcast(I32), 0)
-        load_scale_rows(nc.gpsimd, w3s_raw, w3_scales[0])
         nc.sync.dma_start(offs_sb[:], offs)
         nc.sync.dma_start(out=w1_raw[:], in_=w1.rearrange("(p j) c -> p j c", j=PACK))
         nc.sync.dma_start(la_sb[:], la)
@@ -57,8 +54,8 @@ def tile_picked_unmerge_relu_po_kernel(
         nc.sync.dma_start(out=xw[:].bitcast(I32), in_=x_words[0].rearrange("p n t -> p (n t)").bitcast(I32))
         load_scale_rows(nc.scalar, xs, x_scales[0])
 
-        def deal(engine, raw, name, pair):
-            grouped = sb(name, [P, 2, P, PACK], BF16)
+        def deal(engine, raw, name, pair, tag=None):
+            grouped = sb(name, [P, 2, P, PACK], BF16, tag)
             dst = grouped[:].rearrange("p t m j -> p m j t")
             src = raw[:].rearrange("p j (m t) -> p m j t", t=PACK)[:, :, :, 2 * pair : 2 * pair + 2]
             if engine is nc.vector:
@@ -83,6 +80,9 @@ def tile_picked_unmerge_relu_po_kernel(
         nc.sync.dma_start(out=w3w_raw[:].bitcast(I32), in_=w3_words[0].bitcast(I32))
         w2_raw = sb("w2_raw", [P, PACK, H], F32, "w_raw")
         nc.sync.dma_start(out=w2_raw[:], in_=w2.rearrange("(p j) c -> p j c", j=PACK))
+        w3s_raw = sb("w3s_raw", [P, N], U8, "w1_g1")
+        nc.gpsimd.memset(w3s_raw[:].bitcast(I32), 0)
+        load_scale_rows(nc.sync, w3s_raw, w3_scales[0])
 
         half = S // 2
         xg = [sb("xg0", [P, half], U32, "xs"), sb("xg1", [P, half], U32)]
@@ -105,7 +105,7 @@ def tile_picked_unmerge_relu_po_kernel(
             )
             nc.scalar.copy(out=y[t][:, half * u : half * u + half], in_=acc[:])
 
-        w3w = sb("w3w", [P, PACK, P, 2], U8)
+        w3w = sb("w3w", [P, PACK, P, 2], U8, "xw")
         w3s = sb("w3s", [P, PACK, P], U8)
         nc.vector.tensor_copy(
             out=w3w[:].rearrange("p t m b -> p m t b"), in_=w3w_raw[:].rearrange("p (m t b) -> p m t b", t=PACK, b=2)
@@ -113,25 +113,17 @@ def tile_picked_unmerge_relu_po_kernel(
         nc.vector.tensor_copy(out=w3s[:].rearrange("p t m -> p m t"), in_=w3s_raw[:].rearrange("p (m t) -> p m t", t=PACK))
 
         vh = V // 2
-        a = [sb(f"a{g}", [P, PACK, vh], F32) for g in range(2)]
         s = [sb(f"s{g}", [P, PACK, vh], F32) for g in range(2)]
         df = sb("df", [P, PACK, V], F32)
         ndf = sb("ndf", [P, PACK, V], F32)
         h = sb("h", [P, PACK, V], F32)
 
-        def gather(g, t):
+        def gathers(g, a, ts):
             lists = slice(8 * g, 8 * g + 8)
-            nc.vector.tensor_copy(out=a[g][:, t, :], in_=y[t][:].indirect(la_sb[:, lists]))
-
-        def gather_add(g, t):
-            lists = slice(8 * g, 8 * g + 8)
-            nc.vector.tensor_tensor(out=s[g][:, t, :], in0=y[t][:].indirect(lb_sb[:, lists]), in1=a[g][:, t, :], op=ALU.add)
-
-        def gathers(g, ts):
-            for t in ts:
-                gather(g, t)
-            for t in ts:
-                gather_add(g, t)
+            for i, t in enumerate(ts):
+                nc.vector.tensor_copy(out=a[:, i, :], in_=y[t][:].indirect(la_sb[:, lists]))
+            for i, t in enumerate(ts):
+                nc.vector.tensor_tensor(out=s[g][:, t, :], in0=y[t][:].indirect(lb_sb[:, lists]), in1=a[:, i, :], op=ALU.add)
 
         def merge(g):
             zi = sb(f"zi{g}", [P, vh, PACK], BF16)
@@ -159,30 +151,35 @@ def tile_picked_unmerge_relu_po_kernel(
                 )
             nc.scalar.activation(out=h[:, :, vh * g : vh * g + vh], in_=acc[:], func=ACT.Relu)
 
-        def difference(g):
+        def difference(g, a, rows):
             cols = slice(vh * g, vh * g + vh)
             nc.vector.scalar_tensor_tensor(
-                out=df[:, :, cols], in0=a[g][:], scalar=2.0, in1=s[g][:], op0=ALU.mult, op1=ALU.subtract
+                out=df[:, rows, cols], in0=a, scalar=2.0, in1=s[g][:, rows, :], op0=ALU.mult, op1=ALU.subtract
             )
 
-        gathers(0, [0, 1])
-        gathers(0, [2, 3])
-        g2a = deal(nc.scalar, w2_raw, "w2_g0", 0)
+        def negate(g):
+            cols = slice(vh * g, vh * g + vh)
+            nc.scalar.activation(out=ndf[:, :, cols], in_=df[:, :, cols], func=ACT.Copy, scale=-1.0)
+
+        a0 = sb("a0", [P, PACK, vh], F32)
+        gathers(0, a0[:, 0:2, :], [0, 1])
+        gathers(0, a0[:, 2:4, :], [2, 3])
+        g2a = deal(nc.scalar, w2_raw, "w2_g0", 0, "xg1")
         zi0 = merge(0)
-        g2b = deal(nc.scalar, w2_raw, "w2_g1", 1)
-        gathers(1, [0, 1])
+        g2b = deal(nc.scalar, w2_raw, "w2_g1", 1, "w1_q1_codes")
+        difference(0, a0[:], slice(0, 4))
+        a1_lo = sb("a1_lo", [P, 2, vh], F32, "a0")
+        gathers(1, a1_lo[:], [0, 1])
         q2a = quantise("w2_q0", g2a[:].rearrange("p t m j -> p (t m j)"), 2 * P)
-        qz0 = quantise("z_q0", zi0[:].rearrange("p v t -> p (v t)"), vh)
-        gathers(1, [2, 3])
         q2b = quantise("w2_q1", g2b[:].rearrange("p t m j -> p (t m j)"), 2 * P)
-        zi1 = merge(1)
+        qz0 = quantise("z_q0", zi0[:].rearrange("p v t -> p (v t)"), vh)
+        a1_hi = sb("a1_hi", [P, 2, vh], F32, "zi0")
+        gathers(1, a1_hi[:], [2, 3])
         second_layer(0, qz0, [q2a, q2b])
-        difference(0)
-        difference(1)
-        qz1 = quantise("z_q1", zi1[:].rearrange("p v t -> p (v t)"), vh)
-        second_layer(1, qz1, [q2a, q2b])
-        for u in range(2):
-            nc.scalar.activation(out=ndf[:, 2 * u : 2 * u + 2, :], in_=df[:, 2 * u : 2 * u + 2, :], func=ACT.Copy, scale=-1.0)
+        zi1 = merge(1)
+        difference(1, a1_lo[:], slice(0, 2))
+        difference(1, a1_hi[:], slice(2, 4))
+        negate(0)
 
         z2 = [sb(f"z2_{t}", [P, S], F32) for t in range(PACK)]
         chunks = S // CHUNK
@@ -198,15 +195,21 @@ def tile_picked_unmerge_relu_po_kernel(
                 nc.scalar.copy(out=z2i[c][:, :, t], in_=z2[t][:, CHUNK * c : CHUNK * c + CHUNK])
 
         scatter(0, la_sb, df, 0, vh)
-        scatter(1, la_sb, df, 0, vh)
+        qz1 = quantise("z_q1", zi1[:].rearrange("p v t -> p (v t)"), vh)
+        second_layer(1, qz1, [q2a, q2b])
+        negate(1)
+        for t in range(1, PACK):
+            scatter(t, la_sb, df, 0, vh)
+        scatter(0, lb_sb, ndf, 0, vh)
+        scatter(1, lb_sb, ndf, 0, vh)
         scatter(0, la_sb, df, vh, V)
         scatter(1, la_sb, df, vh, V)
-        scatter(0, lb_sb, ndf, 0, V)
+        scatter(0, lb_sb, ndf, vh, V)
         weave(0)
-        scatter(2, la_sb, df, 0, V)
-        scatter(1, lb_sb, ndf, 0, V)
+        scatter(2, la_sb, df, vh, V)
+        scatter(1, lb_sb, ndf, vh, V)
         weave(1)
-        scatter(3, la_sb, df, 0, V)
+        scatter(3, la_sb, df, vh, V)
         scatter(2, lb_sb, ndf, 0, V)
         weave(2)
         scatter(3, lb_sb, ndf, 0, V)

@@ -27,6 +27,8 @@ def tile_picked_unmerge_relu_po_kernel(
     nc = tc.nc
     with ExitStack() as ctx:
         keep = ctx.enter_context(tc.tile_pool(name="keep", bufs=1))
+        early = ctx.enter_context(tc.tile_pool(name="early", bufs=1))
+        middle = ctx.enter_context(tc.tile_pool(name="middle", bufs=1))
         psum = ctx.enter_context(tc.psum_pool(name="psum", bufs=1))
 
         def sb(name, shape, dtype, tag=None):
@@ -43,7 +45,7 @@ def tile_picked_unmerge_relu_po_kernel(
         la_sb = keep.tile([P, V // 16], U16, name="la_sb")
         lb_sb = keep.tile([P, V // 16], U16, name="lb_sb")
         xw = sb("xw", [P, T], U32)
-        xs = sb("xs", [P, T], U8)
+        xs = early.tile([P, T], U8, name="xs", align_bytes=64, offset=0)
         w1_raw = sb("w1_raw", [P, PACK, H], F32, "w_raw")
 
         nc.vector.memset(xs[:].bitcast(I32), 0)
@@ -64,30 +66,33 @@ def tile_picked_unmerge_relu_po_kernel(
                 nc.scalar.copy(out=dst, in_=src)
             return grouped
 
-        def quantise(name, values, width):
-            codes = sb(name + "_codes", [P, width], U32)
+        def quantise(name, values, width, codes=None):
+            if codes is None:
+                codes = sb(name + "_codes", [P, width], U32)
             scales = sb(name + "_scales", [P, width], U8)
             nc.vector.quantize_mx(out=codes[:].bitcast(FP8X4), scales=scales[:], in_=values)
             return codes, scales
 
         xsg = sb("xsg", [P, S], U8)
-        g1 = [deal(nc.vector, w1_raw, "w1_g0", 0), deal(nc.scalar, w1_raw, "w1_g1", 1)]
-        q1 = [quantise("w1_q0", g1[0][:].rearrange("p t m j -> p (t m j)"), 2 * P)]
         nc.vector.tensor_copy(out=xsg[:], in_=xs[:].indirect(offs_sb[:]))
-        q1.append(quantise("w1_q1", g1[1][:].rearrange("p t m j -> p (t m j)"), 2 * P))
+        g1 = [deal(nc.scalar, w1_raw, "w1_g0", 0), deal(nc.scalar, w1_raw, "w1_g1", 1)]
+        w1_codes = early.tile([P, 2 * P], U32, name="w1_q0_codes", align_bytes=64, offset=0)
+        q1 = [quantise("w1_q0", g1[0][:].rearrange("p t m j -> p (t m j)"), 2 * P, w1_codes)]
 
-        w3w_raw = sb("w3w_raw", [P, 2 * N], U8, "w1_g0")
+        w3w_raw = early.tile([P, 2 * N], U8, name="w3w_raw", align_bytes=64, offset=1024)
         nc.sync.dma_start(out=w3w_raw[:].bitcast(I32), in_=w3_words[0].bitcast(I32))
         w2_raw = sb("w2_raw", [P, PACK, H], F32, "w_raw")
         nc.sync.dma_start(out=w2_raw[:], in_=w2.rearrange("(p j) c -> p j c", j=PACK))
+
+        half = S // 2
+        xg = [sb("xg0", [P, half], U32, "w1_g0"), middle.tile([P, half], U32, name="xg1", align_bytes=64, offset=0)]
+        for u in range(2):
+            nc.vector.tensor_copy(out=xg[u][:], in_=xw[:].indirect(offs_sb[:, 16 * u : 16 * u + 16]))
+
+        q1.append(quantise("w1_q1", g1[1][:].rearrange("p t m j -> p (t m j)"), 2 * P))
         w3s_raw = sb("w3s_raw", [P, N], U8, "w1_g1")
         nc.gpsimd.memset(w3s_raw[:].bitcast(I32), 0)
         load_scale_rows(nc.sync, w3s_raw, w3_scales[0])
-
-        half = S // 2
-        xg = [sb("xg0", [P, half], U32, "xs"), sb("xg1", [P, half], U32)]
-        for u in range(2):
-            nc.vector.tensor_copy(out=xg[u][:], in_=xw[:].indirect(offs_sb[:, 16 * u : 16 * u + 16]))
 
         y = [sb(f"y{t}", [P, S], F32) for t in range(PACK)]
         for t, u in [(0, 0), (1, 0), (0, 1), (1, 1), (2, 0), (2, 1), (3, 0), (3, 1)]:
@@ -103,117 +108,74 @@ def tile_picked_unmerge_relu_po_kernel(
                 start=True,
                 stop=True,
             )
-            nc.scalar.copy(out=y[t][:, half * u : half * u + half], in_=acc[:])
+            nc.scalar.activation(out=y[t][:, half * u : half * u + half], in_=acc[:], func=ACT.Copy, scale=0.75)
 
         w3w = sb("w3w", [P, PACK, P, 2], U8, "xw")
-        w3s = sb("w3s", [P, PACK, P], U8)
         nc.vector.tensor_copy(
             out=w3w[:].rearrange("p t m b -> p m t b"), in_=w3w_raw[:].rearrange("p (m t b) -> p m t b", t=PACK, b=2)
         )
+
+        a = sb("a", [P, PACK, V], F32)
+        b = sb("b", [P, PACK, V], F32)
+        for t in range(PACK):
+            nc.vector.tensor_copy(out=a[:, t, :], in_=y[t][:].indirect(la_sb[:]))
+            nc.vector.tensor_copy(out=b[:, t, :], in_=y[t][:].indirect(lb_sb[:]))
+
+        g2 = middle.tile([P, PACK, P, PACK], BF16, name="w2_g", align_bytes=64, offset=0)
+        nc.scalar.copy(out=g2[:].rearrange("p t m j -> p m j t"), in_=w2_raw[:].rearrange("p j (m t) -> p m j t", t=PACK))
+        w2_codes, w2_scales = quantise("w2_q", g2[:].rearrange("p t m j -> p (t m j)"), H)
+
+        zi = middle.tile([P, V, PACK], BF16, name="zi", align_bytes=64, offset=0)
+        nc.vector.tensor_tensor(
+            out=zi[:].rearrange("p (c i) t -> p c t i", i=4),
+            in0=a[:].rearrange("p t (c i) -> p c t i", i=4),
+            in1=b[:].rearrange("p t (c i) -> p c t i", i=4),
+            op=ALU.add,
+        )
+        z_codes, z_scales = quantise("z_q", zi[:].rearrange("p v t -> p (v t)"), V)
+        d = middle.tile([P, PACK, V], F32, name="d", align_bytes=64, offset=1024)
+        for rows in (slice(0, 1), slice(1, PACK)):
+            nc.vector.tensor_tensor(out=d[:, rows, :], in0=a[:, rows, :], in1=b[:, rows, :], op=ALU.subtract)
+        w3s = middle.tile([P, PACK, P], U8, name="w3s", align_bytes=64, offset=0)
         nc.vector.tensor_copy(out=w3s[:].rearrange("p t m -> p m t"), in_=w3s_raw[:].rearrange("p (m t) -> p m t", t=PACK))
 
-        vh = V // 2
-        s = [sb(f"s{g}", [P, PACK, vh], F32) for g in range(2)]
+        h = sb("h", [P, PACK, V], F32)
         df = sb("df", [P, PACK, V], F32)
         ndf = sb("ndf", [P, PACK, V], F32)
-        h = sb("h", [P, PACK, V], F32)
-
-        def gathers(g, a, ts):
-            lists = slice(8 * g, 8 * g + 8)
-            for i, t in enumerate(ts):
-                nc.vector.tensor_copy(out=a[:, i, :], in_=y[t][:].indirect(la_sb[:, lists]))
-            for i, t in enumerate(ts):
-                nc.vector.tensor_tensor(out=s[g][:, t, :], in0=y[t][:].indirect(lb_sb[:, lists]), in1=a[:, i, :], op=ALU.add)
-
-        def merge(g):
-            zi = sb(f"zi{g}", [P, vh, PACK], BF16)
-            nc.scalar.activation(
-                out=zi[:].rearrange("p (c i) t -> p c t i", i=4),
-                in_=s[g][:].rearrange("p t (c i) -> p c t i", i=4),
-                func=ACT.Copy,
-                scale=0.75,
+        for t in range(PACK):
+            acc = bank(t, f"h_acc{t}", [P, V])
+            nc.tensor.matmul_mx(
+                out=acc[:],
+                lhsT=w2_codes[:, P * t : P * t + P].bitcast(FP8X4),
+                lhsT_scale=w2_scales[:, P * t : P * t + P],
+                rhs=z_codes[:].bitcast(FP8X4),
+                rhs_scale=z_scales[:],
+                start=True,
+                stop=True,
             )
-            return zi
-
-        def second_layer(g, qz, q2):
-            acc = bank(g, f"h_acc{g}", [P, PACK, vh])
-            for t in range(PACK):
-                codes, scales = q2[t // 2]
-                cols = slice(P * (t % 2), P * (t % 2) + P)
-                nc.tensor.matmul_mx(
-                    out=acc[:, t, :],
-                    lhsT=codes[:, cols].bitcast(FP8X4),
-                    lhsT_scale=scales[:, cols],
-                    rhs=qz[0][:].bitcast(FP8X4),
-                    rhs_scale=qz[1][:],
-                    start=True,
-                    stop=True,
-                )
-            nc.scalar.activation(out=h[:, :, vh * g : vh * g + vh], in_=acc[:], func=ACT.Relu)
-
-        def difference(g, a, rows):
-            cols = slice(vh * g, vh * g + vh)
-            nc.vector.scalar_tensor_tensor(
-                out=df[:, rows, cols], in0=a, scalar=2.0, in1=s[g][:, rows, :], op0=ALU.mult, op1=ALU.subtract
-            )
-
-        def negate(g):
-            cols = slice(vh * g, vh * g + vh)
-            nc.scalar.activation(out=ndf[:, :, cols], in_=df[:, :, cols], func=ACT.Copy, scale=-1.0)
-
-        a0 = sb("a0", [P, PACK, vh], F32)
-        gathers(0, a0[:, 0:2, :], [0, 1])
-        gathers(0, a0[:, 2:4, :], [2, 3])
-        g2a = deal(nc.scalar, w2_raw, "w2_g0", 0, "xg1")
-        zi0 = merge(0)
-        g2b = deal(nc.scalar, w2_raw, "w2_g1", 1, "w1_q1_codes")
-        difference(0, a0[:], slice(0, 4))
-        a1_lo = sb("a1_lo", [P, 2, vh], F32, "a0")
-        gathers(1, a1_lo[:], [0, 1])
-        q2a = quantise("w2_q0", g2a[:].rearrange("p t m j -> p (t m j)"), 2 * P)
-        q2b = quantise("w2_q1", g2b[:].rearrange("p t m j -> p (t m j)"), 2 * P)
-        qz0 = quantise("z_q0", zi0[:].rearrange("p v t -> p (v t)"), vh)
-        a1_hi = sb("a1_hi", [P, 2, vh], F32, "zi0")
-        gathers(1, a1_hi[:], [2, 3])
-        second_layer(0, qz0, [q2a, q2b])
-        zi1 = merge(1)
-        difference(1, a1_lo[:], slice(0, 2))
-        difference(1, a1_hi[:], slice(2, 4))
-        negate(0)
+            nc.scalar.activation(out=h[:, t, :], in_=acc[:], func=ACT.Relu)
+            nc.scalar.activation(out=df[:, t, :], in_=d[:, t, :], func=ACT.Copy, scale=4.0 / 3.0)
+            if t > 0:
+                nc.scalar.activation(out=ndf[:, t - 1, :], in_=d[:, t - 1, :], func=ACT.Copy, scale=-4.0 / 3.0)
+        nc.scalar.activation(out=ndf[:, 3, :], in_=d[:, 3, :], func=ACT.Copy, scale=-4.0 / 3.0)
 
         z2 = [sb(f"z2_{t}", [P, S], F32) for t in range(PACK)]
         chunks = S // CHUNK
         z2i = [sb(f"z2i{c}", [P, CHUNK, PACK], BF16) for c in range(chunks)]
 
-        def scatter(t, lists, term, lo, hi):
-            nc.vector.tensor_tensor(
-                out=z2[t][:].indirect(lists[:, lo // 16 : hi // 16]), in0=h[:, t, lo:hi], in1=term[:, t, lo:hi], op=ALU.add
-            )
+        def scatter(t, lists, term):
+            nc.vector.tensor_tensor(out=z2[t][:].indirect(lists[:]), in0=h[:, t, :], in1=term[:, t, :], op=ALU.add)
 
         def weave(t):
             for c in range(chunks):
                 nc.scalar.copy(out=z2i[c][:, :, t], in_=z2[t][:, CHUNK * c : CHUNK * c + CHUNK])
 
-        scatter(0, la_sb, df, 0, vh)
-        qz1 = quantise("z_q1", zi1[:].rearrange("p v t -> p (v t)"), vh)
-        second_layer(1, qz1, [q2a, q2b])
-        negate(1)
-        for t in range(1, PACK):
-            scatter(t, la_sb, df, 0, vh)
-        scatter(0, lb_sb, ndf, 0, vh)
-        scatter(1, lb_sb, ndf, 0, vh)
-        scatter(0, la_sb, df, vh, V)
-        scatter(1, la_sb, df, vh, V)
-        scatter(0, lb_sb, ndf, vh, V)
-        weave(0)
-        scatter(2, la_sb, df, vh, V)
-        scatter(1, lb_sb, ndf, vh, V)
-        weave(1)
-        scatter(3, la_sb, df, vh, V)
-        scatter(2, lb_sb, ndf, 0, V)
-        weave(2)
-        scatter(3, lb_sb, ndf, 0, V)
-        weave(3)
+        scatter(0, la_sb, df)
+        for t in range(PACK):
+            if t + 1 < PACK:
+                scatter(t + 1, la_sb, df)
+            scatter(t, lb_sb, ndf)
+            weave(t)
 
         out_rows = out_0.rearrange("(p t) j -> p t j", t=PACK)
         word_rows = out_1[0].rearrange("p n t -> p (n t)").bitcast(I32)
@@ -222,10 +184,13 @@ def tile_picked_unmerge_relu_po_kernel(
         qz2 = [quantise(f"z2_q{c}", z2i[c][:].rearrange("p v t -> p (v t)"), CHUNK) for c in range(chunks)]
         for c in range(chunks):
             cols = slice(CHUNK * c, CHUNK * c + CHUNK)
-            acc = bank(2 + c, f"o_acc{c}", [P, PACK, CHUNK])
+            o = sb(f"o{c}", [P, PACK, CHUNK], F32)
+            per_bank = 2 if c == chunks - 1 else PACK
             for t in range(PACK):
+                if t % per_bank == 0:
+                    acc = bank(2 + c + t // per_bank, f"o_acc{c}_{t}", [P, per_bank, CHUNK])
                 nc.tensor.matmul_mx(
-                    out=acc[:, t, :],
+                    out=acc[:, t % per_bank, :],
                     lhsT=w3w[:, t, :, :].rearrange("p m b -> p (m b)").bitcast(FP4X4),
                     lhsT_scale=w3s[:, t, :],
                     rhs=qz2[c][0][:].bitcast(FP8X4),
@@ -233,8 +198,8 @@ def tile_picked_unmerge_relu_po_kernel(
                     start=True,
                     stop=True,
                 )
-            o = sb(f"o{c}", [P, PACK, CHUNK], F32)
-            nc.scalar.copy(out=o[:], in_=acc[:])
+                if t % per_bank == per_bank - 1:
+                    nc.scalar.copy(out=o[:, t + 1 - per_bank : t + 1, :], in_=acc[:])
             nc.sync.dma_start(out=out_rows[:, :, cols], in_=o[:])
             oi = sb(f"oi{c}", [P, CHUNK, PACK], BF16)
             nc.vector.tensor_copy(

@@ -85,17 +85,14 @@ def tile_picked_unmerge_relu_po_kernel(
         nc.sync.dma_start(out=w2_raw[:], in_=w2.rearrange("(p j) c -> p j c", j=PACK))
 
         half = S // 2
-        xg = [sb("xg0", [P, half], U32, "w1_g0"), middle.tile([P, half], U32, name="xg1", align_bytes=64, offset=0)]
+        xg = [sb("xg0", [P, half], U32, "w1_g0"), middle.tile([P, half], U32, name="xg1", align_bytes=64, offset=4096)]
         for u in range(2):
             nc.vector.tensor_copy(out=xg[u][:], in_=xw[:].indirect(offs_sb[:, 16 * u : 16 * u + 16]))
 
         q1.append(quantise("w1_q1", g1[1][:].rearrange("p t m j -> p (t m j)"), 2 * P))
-        w3s_raw = sb("w3s_raw", [P, N], U8, "w1_g1")
-        nc.gpsimd.memset(w3s_raw[:].bitcast(I32), 0)
-        load_scale_rows(nc.sync, w3s_raw, w3_scales[0])
 
         y = [sb(f"y{t}", [P, S], F32) for t in range(PACK)]
-        for t, u in [(0, 0), (1, 0), (0, 1), (1, 1), (2, 0), (2, 1), (3, 0), (3, 1)]:
+        for t, u in [(t, u) for t in range(PACK) for u in range(2)]:
             codes, scales = q1[t // 2]
             cols = slice(P * (t % 2), P * (t % 2) + P)
             acc = bank(2 * t + u, f"y_acc{t}{u}", [P, half])
@@ -110,10 +107,18 @@ def tile_picked_unmerge_relu_po_kernel(
             )
             nc.scalar.activation(out=y[t][:, half * u : half * u + half], in_=acc[:], func=ACT.Copy, scale=0.75)
 
-        w3w = sb("w3w", [P, PACK, P, 2], U8, "xw")
-        nc.vector.tensor_copy(
-            out=w3w[:].rearrange("p t m b -> p m t b"), in_=w3w_raw[:].rearrange("p (m t b) -> p m t b", t=PACK, b=2)
-        )
+        w3s_raw = sb("w3s_raw", [P, N], U8, "w1_g0")
+        nc.gpsimd.memset(w3s_raw[:].bitcast(I32), 0)
+        load_scale_rows(nc.sync, w3s_raw, w3_scales[0])
+
+        def deal_w3(dealt, pair):
+            nc.vector.tensor_copy(
+                out=dealt[:].rearrange("p t m b -> p m t b"),
+                in_=w3w_raw[:].rearrange("p (m t b) -> p m t b", t=PACK, b=2)[:, :, 2 * pair : 2 * pair + 2, :],
+            )
+
+        w3w = [sb("w3w0", [P, 2, P, 2], U8, "xw")]
+        deal_w3(w3w[0], 0)
 
         a = sb("a", [P, PACK, V], F32)
         b = sb("b", [P, PACK, V], F32)
@@ -121,27 +126,27 @@ def tile_picked_unmerge_relu_po_kernel(
             nc.vector.tensor_copy(out=a[:, t, :], in_=y[t][:].indirect(la_sb[:]))
             nc.vector.tensor_copy(out=b[:, t, :], in_=y[t][:].indirect(lb_sb[:]))
 
-        g2 = middle.tile([P, PACK, P, PACK], BF16, name="w2_g", align_bytes=64, offset=0)
+        g2 = middle.tile([P, PACK, P, PACK], BF16, name="w2_g", align_bytes=64, offset=4096)
         nc.scalar.copy(out=g2[:].rearrange("p t m j -> p m j t"), in_=w2_raw[:].rearrange("p j (m t) -> p m j t", t=PACK))
-        w2_codes, w2_scales = quantise("w2_q", g2[:].rearrange("p t m j -> p (t m j)"), H)
-
-        zi = middle.tile([P, V, PACK], BF16, name="zi", align_bytes=64, offset=0)
+        zi = sb("zi", [P, V, PACK], BF16)
         nc.vector.tensor_tensor(
             out=zi[:].rearrange("p (c i) t -> p c t i", i=4),
             in0=a[:].rearrange("p t (c i) -> p c t i", i=4),
             in1=b[:].rearrange("p t (c i) -> p c t i", i=4),
             op=ALU.add,
         )
-        z_codes, z_scales = quantise("z_q", zi[:].rearrange("p v t -> p (v t)"), V)
+        w2_codes, w2_scales = quantise("w2_q", g2[:].rearrange("p t m j -> p (t m j)"), H)
+        z_codes = middle.tile([P, V], U32, name="z_codes", align_bytes=64, offset=5632)
+        z_codes, z_scales = quantise("z_q", zi[:].rearrange("p v t -> p (v t)"), V, z_codes)
         d = middle.tile([P, PACK, V], F32, name="d", align_bytes=64, offset=1024)
         for rows in (slice(0, 1), slice(1, PACK)):
             nc.vector.tensor_tensor(out=d[:, rows, :], in0=a[:, rows, :], in1=b[:, rows, :], op=ALU.subtract)
-        w3s = middle.tile([P, PACK, P], U8, name="w3s", align_bytes=64, offset=0)
-        nc.vector.tensor_copy(out=w3s[:].rearrange("p t m -> p m t"), in_=w3s_raw[:].rearrange("p (m t) -> p m t", t=PACK))
+        w3w.append(middle.tile([P, 2, P, 2], U8, name="w3w1", align_bytes=64, offset=5120))
+        deal_w3(w3w[1], 1)
 
         h = sb("h", [P, PACK, V], F32)
         df = sb("df", [P, PACK, V], F32)
-        ndf = sb("ndf", [P, PACK, V], F32)
+        ndf = [sb(f"ndf{t}", [P, V], F32) for t in range(PACK)]
         for t in range(PACK):
             acc = bank(t, f"h_acc{t}", [P, V])
             nc.tensor.matmul_mx(
@@ -156,25 +161,36 @@ def tile_picked_unmerge_relu_po_kernel(
             nc.scalar.activation(out=h[:, t, :], in_=acc[:], func=ACT.Relu)
             nc.scalar.activation(out=df[:, t, :], in_=d[:, t, :], func=ACT.Copy, scale=4.0 / 3.0)
             if t > 0:
-                nc.scalar.activation(out=ndf[:, t - 1, :], in_=d[:, t - 1, :], func=ACT.Copy, scale=-4.0 / 3.0)
-        nc.scalar.activation(out=ndf[:, 3, :], in_=d[:, 3, :], func=ACT.Copy, scale=-4.0 / 3.0)
+                nc.scalar.activation(out=ndf[t - 1][:], in_=d[:, t - 1, :], func=ACT.Copy, scale=-4.0 / 3.0)
+        nc.scalar.activation(out=ndf[3][:], in_=d[:, 3, :], func=ACT.Copy, scale=-4.0 / 3.0)
 
         z2 = [sb(f"z2_{t}", [P, S], F32) for t in range(PACK)]
         chunks = S // CHUNK
         z2i = [sb(f"z2i{c}", [P, CHUNK, PACK], BF16) for c in range(chunks)]
 
         def scatter(t, lists, term):
-            nc.vector.tensor_tensor(out=z2[t][:].indirect(lists[:]), in0=h[:, t, :], in1=term[:, t, :], op=ALU.add)
+            nc.vector.tensor_tensor(out=z2[t][:].indirect(lists[:]), in0=h[:, t, :], in1=term, op=ALU.add)
 
         def weave(t):
             for c in range(chunks):
-                nc.scalar.copy(out=z2i[c][:, :, t], in_=z2[t][:, CHUNK * c : CHUNK * c + CHUNK])
+                src = z2[t][:, CHUNK * c : CHUNK * c + CHUNK]
+                if t < 2:
+                    nc.scalar.copy(out=z2i[c][:, :, t], in_=src)
+                elif t == 2:
+                    nc.scalar.copy(out=z2i[c][:, :, 2:4], in_=src.unsqueeze(2).to_broadcast([P, CHUNK, 2]))
+                else:
+                    nc.vector.tensor_copy(out=z2i[c][:, :, t], in_=src)
 
-        scatter(0, la_sb, df)
+        scatter(0, la_sb, df[:, 0, :])
         for t in range(PACK):
             if t + 1 < PACK:
-                scatter(t + 1, la_sb, df)
-            scatter(t, lb_sb, ndf)
+                scatter(t + 1, la_sb, df[:, t + 1, :])
+            scatter(t, lb_sb, ndf[t][:])
+            if t == PACK - 1:
+                w3s = sb("w3s", [P, PACK, P], U8, "ndf2")
+                nc.vector.tensor_copy(
+                    out=w3s[:].rearrange("p t m -> p m t"), in_=w3s_raw[:].rearrange("p (m t) -> p m t", t=PACK)
+                )
             weave(t)
 
         out_rows = out_0.rearrange("(p t) j -> p t j", t=PACK)
@@ -191,7 +207,7 @@ def tile_picked_unmerge_relu_po_kernel(
                     acc = bank(2 + c + t // per_bank, f"o_acc{c}_{t}", [P, per_bank, CHUNK])
                 nc.tensor.matmul_mx(
                     out=acc[:, t % per_bank, :],
-                    lhsT=w3w[:, t, :, :].rearrange("p m b -> p (m b)").bitcast(FP4X4),
+                    lhsT=w3w[t // 2][:, t % 2, :, :].rearrange("p m b -> p (m b)").bitcast(FP4X4),
                     lhsT_scale=w3s[:, t, :],
                     rhs=qz2[c][0][:].bitcast(FP8X4),
                     rhs_scale=qz2[c][1][:],
@@ -201,14 +217,20 @@ def tile_picked_unmerge_relu_po_kernel(
                 if t % per_bank == per_bank - 1:
                     nc.scalar.copy(out=o[:, t + 1 - per_bank : t + 1, :], in_=acc[:])
             nc.sync.dma_start(out=out_rows[:, :, cols], in_=o[:])
-            oi = sb(f"oi{c}", [P, CHUNK, PACK], BF16)
+            if c < chunks - 1:
+                width = CHUNK if c < chunks - 2 else 2 * CHUNK
+                first = CHUNK * c
+                oi = sb(f"oi{c}", [P, width, PACK], BF16)
             nc.vector.tensor_copy(
-                out=oi[:].rearrange("p (c i) t -> p c t i", i=4), in_=o[:].rearrange("p t (c i) -> p c t i", i=4)
+                out=oi[:, CHUNK * c - first : CHUNK * c - first + CHUNK, :].rearrange("p (c i) t -> p c t i", i=4),
+                in_=o[:].rearrange("p t (c i) -> p c t i", i=4),
             )
-            nc.vector.quantize_mx(
-                out=o_codes[:, cols].bitcast(FP8X4), scales=o_scales[:, cols], in_=oi[:].rearrange("p v t -> p (v t)")
-            )
-            nc.sync.dma_start(out=word_rows[:, cols], in_=o_codes[:, cols].bitcast(I32))
+            if c != chunks - 2:
+                done = slice(first, first + width)
+                nc.vector.quantize_mx(
+                    out=o_codes[:, done].bitcast(FP8X4), scales=o_scales[:, done], in_=oi[:].rearrange("p v t -> p (v t)")
+                )
+                nc.sync.dma_start(out=word_rows[:, done], in_=o_codes[:, done].bitcast(I32))
         for q in range(4):
             queue = nc.sync if q % 2 == 0 else nc.scalar
             queue.dma_start(

@@ -27,7 +27,6 @@ def tile_picked_unmerge_relu_po_kernel(
     nc = tc.nc
     with ExitStack() as ctx:
         keep = ctx.enter_context(tc.tile_pool(name="keep", bufs=1))
-        early = ctx.enter_context(tc.tile_pool(name="early", bufs=1))
         middle = ctx.enter_context(tc.tile_pool(name="middle", bufs=1))
         psum = ctx.enter_context(tc.psum_pool(name="psum", bufs=1))
 
@@ -44,17 +43,23 @@ def tile_picked_unmerge_relu_po_kernel(
         offs_sb = keep.tile([P, S // 16], U16, name="offs_sb")
         la_sb = keep.tile([P, V // 16], U16, name="la_sb")
         lb_sb = keep.tile([P, V // 16], U16, name="lb_sb")
-        xw = sb("xw", [P, T], U32)
-        xs = early.tile([P, T], U8, name="xs", align_bytes=64, offset=0)
+        w3w_raw = sb("w3w_raw", [P, 2 * N], U8, "xw")
+        xs = sb("xs", [P, T], U8)
         w1_raw = sb("w1_raw", [P, PACK, H], F32, "w_raw")
 
         nc.vector.memset(xs[:].bitcast(I32), 0)
         nc.sync.dma_start(offs_sb[:], offs)
+        nc.sync.dma_start(out=w3w_raw[:].bitcast(I32), in_=w3_words[0].bitcast(I32))
         nc.sync.dma_start(out=w1_raw[:], in_=w1.rearrange("(p j) c -> p j c", j=PACK))
         nc.sync.dma_start(la_sb[:], la)
         nc.sync.dma_start(lb_sb[:], lb)
-        nc.sync.dma_start(out=xw[:].bitcast(I32), in_=x_words[0].rearrange("p n t -> p (n t)").bitcast(I32))
         load_scale_rows(nc.scalar, xs, x_scales[0])
+        w3w = sb("w3w", [P, PACK, P, 2], U8)
+        nc.vector.tensor_copy(
+            out=w3w[:].rearrange("p t m b -> p m t b"), in_=w3w_raw[:].rearrange("p (m t b) -> p m t b", t=PACK, b=2)
+        )
+        xw = sb("xw", [P, T], U32)
+        nc.sync.dma_start(out=xw[:].bitcast(I32), in_=x_words[0].rearrange("p n t -> p (n t)").bitcast(I32))
 
         def deal(engine, raw, name, pair, tag=None):
             grouped = sb(name, [P, 2, P, PACK], BF16, tag)
@@ -76,11 +81,9 @@ def tile_picked_unmerge_relu_po_kernel(
         xsg = sb("xsg", [P, S], U8)
         nc.vector.tensor_copy(out=xsg[:], in_=xs[:].indirect(offs_sb[:]))
         g1 = [deal(nc.scalar, w1_raw, "w1_g0", 0), deal(nc.scalar, w1_raw, "w1_g1", 1)]
-        w1_codes = early.tile([P, 2 * P], U32, name="w1_q0_codes", align_bytes=64, offset=0)
+        w1_codes = sb("w1_q0_codes", [P, 2 * P], U32, "xs")
         q1 = [quantise("w1_q0", g1[0][:].rearrange("p t m j -> p (t m j)"), 2 * P, w1_codes)]
 
-        w3w_raw = early.tile([P, 2 * N], U8, name="w3w_raw", align_bytes=64, offset=1024)
-        nc.sync.dma_start(out=w3w_raw[:].bitcast(I32), in_=w3_words[0].bitcast(I32))
         w2_raw = sb("w2_raw", [P, PACK, H], F32, "w_raw")
         nc.sync.dma_start(out=w2_raw[:], in_=w2.rearrange("(p j) c -> p j c", j=PACK))
 
@@ -111,15 +114,6 @@ def tile_picked_unmerge_relu_po_kernel(
         nc.gpsimd.memset(w3s_raw[:].bitcast(I32), 0)
         load_scale_rows(nc.sync, w3s_raw, w3_scales[0])
 
-        def deal_w3(dealt, pair):
-            nc.vector.tensor_copy(
-                out=dealt[:].rearrange("p t m b -> p m t b"),
-                in_=w3w_raw[:].rearrange("p (m t b) -> p m t b", t=PACK, b=2)[:, :, 2 * pair : 2 * pair + 2, :],
-            )
-
-        w3w = [sb("w3w0", [P, 2, P, 2], U8, "xw")]
-        deal_w3(w3w[0], 0)
-
         a = sb("a", [P, PACK, V], F32)
         b = sb("b", [P, PACK, V], F32)
         for t in range(PACK):
@@ -136,13 +130,11 @@ def tile_picked_unmerge_relu_po_kernel(
             op=ALU.add,
         )
         w2_codes, w2_scales = quantise("w2_q", g2[:].rearrange("p t m j -> p (t m j)"), H)
-        z_codes = middle.tile([P, V], U32, name="z_codes", align_bytes=64, offset=5632)
+        z_codes = middle.tile([P, V], U32, name="z_codes", align_bytes=64, offset=5120)
         z_codes, z_scales = quantise("z_q", zi[:].rearrange("p v t -> p (v t)"), V, z_codes)
         d = middle.tile([P, PACK, V], F32, name="d", align_bytes=64, offset=1024)
         for rows in (slice(0, 1), slice(1, PACK)):
             nc.vector.tensor_tensor(out=d[:, rows, :], in0=a[:, rows, :], in1=b[:, rows, :], op=ALU.subtract)
-        w3w.append(middle.tile([P, 2, P, 2], U8, name="w3w1", align_bytes=64, offset=5120))
-        deal_w3(w3w[1], 1)
 
         h = sb("h", [P, PACK, V], F32)
         df = sb("df", [P, PACK, V], F32)
@@ -207,7 +199,7 @@ def tile_picked_unmerge_relu_po_kernel(
                     acc = bank(2 + c + t // per_bank, f"o_acc{c}_{t}", [P, per_bank, CHUNK])
                 nc.tensor.matmul_mx(
                     out=acc[:, t % per_bank, :],
-                    lhsT=w3w[t // 2][:, t % 2, :, :].rearrange("p m b -> p (m b)").bitcast(FP4X4),
+                    lhsT=w3w[:, t, :, :].rearrange("p m b -> p (m b)").bitcast(FP4X4),
                     lhsT_scale=w3s[:, t, :],
                     rhs=qz2[c][0][:].bitcast(FP8X4),
                     rhs_scale=qz2[c][1][:],

from contextlib import ExitStack

import concourse.mybir as mybir

K, T, S, V, N, H = 512, 2048, 512, 256, 512, 512
FLOPS = 2 * K * H * S + 2 * H * H * V + 2 * H * N * S

F32 = mybir.dt.float32
BF16 = mybir.dt.bfloat16
I32 = mybir.dt.int32
U32 = mybir.dt.uint32
U16 = mybir.dt.uint16
U8 = mybir.dt.uint8
FP8X4 = mybir.dt.float8_e4m3fn_x4
FP4X4 = mybir.dt.float4_e2m1fn_x4
ALU = mybir.AluOpType
ACT = mybir.ActivationFunctionType

P = 128
PACK = 4
CHUNK = 128


def tile_picked_unmerge_relu_po_kernel(
    tc, x_words, x_scales, w1, w2, w3_words, w3_scales, offs, la, lb, out_0, out_1, out_2
):
    nc = tc.nc
    with ExitStack() as ctx:
        keep = ctx.enter_context(tc.tile_pool(name="keep", bufs=1))
        middle = ctx.enter_context(tc.tile_pool(name="middle", bufs=1))
        psum = ctx.enter_context(tc.psum_pool(name="psum", bufs=1))

        def sb(name, shape, dtype, tag=None):
            return keep.tile(shape, dtype, name=name, tag=tag or name, align_bytes=64)

        def bank(number, name, shape):
            return psum.tile(shape, F32, name=name, tag=f"bank{number}")

        def load_scale_rows(queue, tile, rows):
            for q in range(4):
                queue.dma_start(out=tile[32 * q : 32 * q + 4, :].bitcast(I32), in_=rows[4 * q : 4 * q + 4, :].bitcast(I32))

        offs_sb = keep.tile([P, S // 16], U16, name="offs_sb")
        la_sb = keep.tile([P, V // 16], U16, name="la_sb")
        lb_sb = keep.tile([P, V // 16], U16, name="lb_sb")
        w3w_raw = sb("w3w_raw", [P, 2 * N], U8, "xw")
        xs = sb("xs", [P, T], U8)
        w1_raw = sb("w1_raw", [P, PACK, H], F32, "w_raw")

        nc.vector.memset(xs[:].bitcast(I32), 0)
        nc.sync.dma_start(offs_sb[:], offs)
        nc.sync.dma_start(out=w3w_raw[:].bitcast(I32), in_=w3_words[0].bitcast(I32))
        nc.sync.dma_start(out=w1_raw[:], in_=w1.rearrange("(p j) c -> p j c", j=PACK))
        nc.sync.dma_start(la_sb[:], la)
        nc.sync.dma_start(lb_sb[:], lb)
        load_scale_rows(nc.scalar, xs, x_scales[0])
        w3w = sb("w3w", [P, PACK, P, 2], U8)
        nc.vector.tensor_copy(
            out=w3w[:].rearrange("p t m b -> p m t b"), in_=w3w_raw[:].rearrange("p (m t b) -> p m t b", t=PACK, b=2)
        )
        xw = sb("xw", [P, T], U32)
        nc.sync.dma_start(out=xw[:].bitcast(I32), in_=x_words[0].rearrange("p n t -> p (n t)").bitcast(I32))

        def deal(engine, raw, name, pair, tag=None):
            grouped = sb(name, [P, 2, P, PACK], BF16, tag)
            dst = grouped[:].rearrange("p t m j -> p m j t")
            src = raw[:].rearrange("p j (m t) -> p m j t", t=PACK)[:, :, :, 2 * pair : 2 * pair + 2]
            if engine is nc.vector:
                nc.vector.tensor_copy(out=dst, in_=src)
            else:
                nc.scalar.copy(out=dst, in_=src)
            return grouped

        def quantise(name, values, width, codes=None):
            if codes is None:
                codes = sb(name + "_codes", [P, width], U32)
            scales = sb(name + "_scales", [P, width], U8)
            nc.vector.quantize_mx(out=codes[:].bitcast(FP8X4), scales=scales[:], in_=values)
            return codes, scales

        xsg = sb("xsg", [P, S], U8)
        nc.vector.tensor_copy(out=xsg[:], in_=xs[:].indirect(offs_sb[:]))
        g1 = [deal(nc.scalar, w1_raw, "w1_g0", 0), deal(nc.scalar, w1_raw, "w1_g1", 1)]
        w1_codes = sb("w1_q0_codes", [P, 2 * P], U32, "xs")
        q1 = [quantise("w1_q0", g1[0][:].rearrange("p t m j -> p (t m j)"), 2 * P, w1_codes)]

        w2_raw = sb("w2_raw", [P, PACK, H], F32, "w_raw")
        nc.sync.dma_start(out=w2_raw[:], in_=w2.rearrange("(p j) c -> p j c", j=PACK))

        half = S // 2
        xg = [sb("xg0", [P, half], U32, "w1_g0"), middle.tile([P, half], U32, name="xg1", align_bytes=64, offset=4096)]
        for u in range(2):
            nc.vector.tensor_copy(out=xg[u][:], in_=xw[:].indirect(offs_sb[:, 16 * u : 16 * u + 16]))

        q1.append(quantise("w1_q1", g1[1][:].rearrange("p t m j -> p (t m j)"), 2 * P))

        y = [sb(f"y{t}", [P, S], F32) for t in range(PACK)]
        for t, u in [(t, u) for t in range(PACK) for u in range(2)]:
            codes, scales = q1[t // 2]
            cols = slice(P * (t % 2), P * (t % 2) + P)
            acc = bank(2 * t + u, f"y_acc{t}{u}", [P, half])
            nc.tensor.matmul_mx(
                out=acc[:],
                lhsT=codes[:, cols].bitcast(FP8X4),
                lhsT_scale=scales[:, cols],
                rhs=xg[u][:].bitcast(FP8X4),
                rhs_scale=xsg[:, half * u : half * u + half],
                start=True,
                stop=True,
            )
            nc.scalar.activation(out=y[t][:, half * u : half * u + half], in_=acc[:], func=ACT.Copy, scale=0.75)

        w3s_raw = sb("w3s_raw", [P, N], U8, "w1_g0")
        nc.gpsimd.memset(w3s_raw[:].bitcast(I32), 0)
        load_scale_rows(nc.sync, w3s_raw, w3_scales[0])

        a = sb("a", [P, PACK, V], F32)
        b = sb("b", [P, PACK, V], F32)
        for t in range(PACK):
            nc.vector.tensor_copy(out=a[:, t, :], in_=y[t][:].indirect(la_sb[:]))
            nc.vector.tensor_copy(out=b[:, t, :], in_=y[t][:].indirect(lb_sb[:]))

        g2 = middle.tile([P, PACK, P, PACK], BF16, name="w2_g", align_bytes=64, offset=4096)
        nc.scalar.copy(out=g2[:].rearrange("p t m j -> p m j t"), in_=w2_raw[:].rearrange("p j (m t) -> p m j t", t=PACK))
        zi = sb("zi", [P, V, PACK], BF16)
        nc.vector.tensor_tensor(
            out=zi[:].rearrange("p (c i) t -> p c t i", i=4),
            in0=a[:].rearrange("p t (c i) -> p c t i", i=4),
            in1=b[:].rearrange("p t (c i) -> p c t i", i=4),
            op=ALU.add,
        )
        w2_codes, w2_scales = quantise("w2_q", g2[:].rearrange("p t m j -> p (t m j)"), H)
        z_codes = middle.tile([P, V], U32, name="z_codes", align_bytes=64, offset=5120)
        z_codes, z_scales = quantise("z_q", zi[:].rearrange("p v t -> p (v t)"), V, z_codes)
        d = middle.tile([P, PACK, V], F32, name="d", align_bytes=64, offset=1024)
        for rows in (slice(0, 1), slice(1, PACK)):
            nc.vector.tensor_tensor(out=d[:, rows, :], in0=a[:, rows, :], in1=b[:, rows, :], op=ALU.subtract)

        h = sb("h", [P, PACK, V], F32)
        df = sb("df", [P, PACK, V], F32)
        ndf = [sb(f"ndf{t}", [P, V], F32) for t in range(PACK)]
        for t in range(PACK):
            acc = bank(t, f"h_acc{t}", [P, V])
            nc.tensor.matmul_mx(
                out=acc[:],
                lhsT=w2_codes[:, P * t : P * t + P].bitcast(FP8X4),
                lhsT_scale=w2_scales[:, P * t : P * t + P],
                rhs=z_codes[:].bitcast(FP8X4),
                rhs_scale=z_scales[:],
                start=True,
                stop=True,
            )
            nc.scalar.activation(out=h[:, t, :], in_=acc[:], func=ACT.Relu)
            nc.scalar.activation(out=df[:, t, :], in_=d[:, t, :], func=ACT.Copy, scale=4.0 / 3.0)
            if t > 0:
                nc.scalar.activation(out=ndf[t - 1][:], in_=d[:, t - 1, :], func=ACT.Copy, scale=-4.0 / 3.0)
        nc.scalar.activation(out=ndf[3][:], in_=d[:, 3, :], func=ACT.Copy, scale=-4.0 / 3.0)

        z2 = [sb(f"z2_{t}", [P, S], F32) for t in range(PACK)]
        chunks = S // CHUNK
        z2i = [sb(f"z2i{c}", [P, CHUNK, PACK], BF16) for c in range(chunks)]

        def scatter(t, lists, term):
            nc.vector.tensor_tensor(out=z2[t][:].indirect(lists[:]), in0=h[:, t, :], in1=term, op=ALU.add)

        def weave(t):
            for c in range(chunks):
                src = z2[t][:, CHUNK * c : CHUNK * c + CHUNK]
                if t < 2:
                    nc.scalar.copy(out=z2i[c][:, :, t], in_=src)
                elif t == 2:
                    nc.scalar.copy(out=z2i[c][:, :, 2:4], in_=src.unsqueeze(2).to_broadcast([P, CHUNK, 2]))
                else:
                    nc.vector.tensor_copy(out=z2i[c][:, :, t], in_=src)

        scatter(0, la_sb, df[:, 0, :])
        for t in range(PACK):
            if t + 1 < PACK:
                scatter(t + 1, la_sb, df[:, t + 1, :])
            scatter(t, lb_sb, ndf[t][:])
            if t == PACK - 1:
                w3s = sb("w3s", [P, PACK, P], U8, "ndf2")
                nc.vector.tensor_copy(
                    out=w3s[:].rearrange("p t m -> p m t"), in_=w3s_raw[:].rearrange("p (m t) -> p m t", t=PACK)
                )
            weave(t)

        out_rows = out_0.rearrange("(p t) j -> p t j", t=PACK)
        word_rows = out_1[0].rearrange("p n t -> p (n t)").bitcast(I32)
        o_codes = sb("o_codes", [P, S], U32)
        o_scales = sb("o_scales", [P, S], U8)
        qz2 = [quantise(f"z2_q{c}", z2i[c][:].rearrange("p v t -> p (v t)"), CHUNK) for c in range(chunks)]
        for c in range(chunks):
            cols = slice(CHUNK * c, CHUNK * c + CHUNK)
            o = sb(f"o{c}", [P, PACK, CHUNK], F32)
            per_bank = 2 if c == chunks - 1 else PACK
            for t in range(PACK):
                if t % per_bank == 0:
                    acc = bank(2 + c + t // per_bank, f"o_acc{c}_{t}", [P, per_bank, CHUNK])
                nc.tensor.matmul_mx(
                    out=acc[:, t % per_bank, :],
                    lhsT=w3w[:, t, :, :].rearrange("p m b -> p (m b)").bitcast(FP4X4),
                    lhsT_scale=w3s[:, t, :],
                    rhs=qz2[c][0][:].bitcast(FP8X4),
                    rhs_scale=qz2[c][1][:],
                    start=True,
                    stop=True,
                )
                if t % per_bank == per_bank - 1:
                    nc.scalar.copy(out=o[:, t + 1 - per_bank : t + 1, :], in_=acc[:])
            nc.sync.dma_start(out=out_rows[:, :, cols], in_=o[:])
            if c < chunks - 1:
                width = CHUNK if c < chunks - 2 else 2 * CHUNK
                first = CHUNK * c
                oi = sb(f"oi{c}", [P, width, PACK], BF16)
            nc.vector.tensor_copy(
                out=oi[:, CHUNK * c - first : CHUNK * c - first + CHUNK, :].rearrange("p (c i) t -> p c t i", i=4),
                in_=o[:].rearrange("p t (c i) -> p c t i", i=4),
            )
            if c != chunks - 2:
                done = slice(first, first + width)
                nc.vector.quantize_mx(
                    out=o_codes[:, done].bitcast(FP8X4), scales=o_scales[:, done], in_=oi[:].rearrange("p v t -> p (v t)")
                )
                nc.sync.dma_start(out=word_rows[:, done], in_=o_codes[:, done].bitcast(I32))
        for q in range(4):
            queue = nc.sync if q % 2 == 0 else nc.scalar
            queue.dma_start(
                out=out_2[0][4 * q : 4 * q + 4, :].bitcast(I32), in_=o_scales[32 * q : 32 * q + 4, :].bitcast(I32)
            )
